import numpy as np
import ml_dtypes


def mxq(x, axis, fmt="e4m3"):
    dtype, down = {"e4m3": (ml_dtypes.float8_e4m3fn, 7), "e5m2": (ml_dtypes.float8_e5m2, 14)}[fmt]
    v = np.moveaxis(np.asarray(x, np.float32).astype(ml_dtypes.bfloat16).astype(np.float64), axis, -1)
    blocks = v.reshape(v.shape[:-1] + (-1, 32))
    amax = np.abs(blocks).max(-1, keepdims=True)
    byte = np.maximum(np.where(amax > 0, np.frexp(amax)[1] - 1 + 127, 0) - down, 1)
    scale = np.exp2(byte - 127.0)
    codes = (blocks / scale).astype(np.float32).astype(dtype).astype(np.float64)
    return np.moveaxis((codes * scale).reshape(v.shape), -1, axis)


WIDE = False


def mx_kscale(k):
    if not WIDE:
        return np.ones(k)
    levels = np.array([10, -10, 5, -5, 0])
    if k % 512:
        return np.exp2(np.random.permutation(np.resize(levels, k // 32))).repeat(32)
    a = np.empty((k // 512, 16))
    for p in range(k // 512):
        a[p, :8] = np.random.permutation(np.resize(levels, 8))
        for g in range(8):
            far = levels[np.abs(levels - a[p, g]) >= 10]
            a[p, g + 8] = far[np.random.randint(len(far))]
    return np.exp2(a.ravel()).repeat(32)


def f64(x):
    return np.asarray(x).astype(np.float64)


def striped(idx):
    return np.tile(np.asarray(idx).reshape(-1, 16).T, (8, 1)).astype(np.uint16)


def unstriped(offs):
    return offs[:16].T.reshape(-1).astype(np.int64)


E2M1 = np.array([0.0, 0.5, 1.0, 1.5, 2.0, 3.0, 4.0, 6.0, -0.0, -0.5, -1.0, -1.5, -2.0, -3.0, -4.0, -6.0])


def pack_weight(w, fmt):
    k, n = w.shape
    w = f64(np.asarray(w, np.float32).astype(ml_dtypes.bfloat16)).reshape(k // 32, 32, n)
    amax = np.abs(w).max(1)
    if fmt == "e4m3":
        byte = np.frexp(amax)[1] - 1 + 127 - 7
    else:
        mant, ex = np.frexp(amax / 6.0)
        byte = np.where(mant > 0.5, ex, ex - 1) + 127
    byte = np.clip(np.where(amax > 0, byte, 1), 1, 254)
    scaled = (w * np.exp2(127.0 - byte)[:, None, :]).reshape(k, n).astype(np.float32)
    by_word = np.ascontiguousarray(scaled.reshape(k // 512, 128, 4, n).transpose(0, 1, 3, 2))
    if fmt == "e4m3":
        words = by_word.astype(ml_dtypes.float8_e4m3fn).view(np.uint8)
    else:
        c = by_word.astype(ml_dtypes.float4_e2m1fn).view(np.uint8) & 0xF
        words = (c[..., 0::2] | (c[..., 1::2] << 4)).reshape(k // 512, 128, 2 * n)
    return np.ascontiguousarray(words), np.ascontiguousarray(byte.astype(np.uint8).reshape(k // 512, 16, n))


def unpack_weight(words, scales, fmt):
    g, _, n = scales.shape
    words = np.ascontiguousarray(words).reshape(g, 128, n, -1)
    if fmt == "e4m3":
        vals = words.view(ml_dtypes.float8_e4m3fn).astype(np.float64)
    else:
        nib = np.empty((g, 128, n, 4), np.uint8)
        nib[..., 0::2] = words & 0xF
        nib[..., 1::2] = words >> 4
        vals = E2M1[nib]
    vals = vals * np.repeat(np.exp2(scales.astype(np.float64) - 127.0), 8, axis=1)[..., None]
    return vals.transpose(0, 1, 3, 2).reshape(g * 512, n)


D, T, I, J, G = 512, 2048, 512, 1024, 128


def setup_inputs():
    n = np.random.standard_normal
    idx = np.random.permutation(T)[:I]
    idx2 = np.random.permutation(T)[:J]
    fd = mx_kscale(D)
    entsp = pack_weight(n((D, T)) / fd[:, None], "e4m3")
    return {
        "ment": (n((D, G)) * 1.0 / np.sqrt(D) * fd[:, None]).astype(np.float32),
        "ents_words": entsp[0],
        "ents_scales": entsp[1],
        "comp": (n((D, T)) * 1.5 / np.sqrt(D) * fd[:, None]).astype(np.float32),
        "trust": (np.random.uniform(0.5, 1.5, (1, G))).astype(np.float32),
        "offs": striped(idx),
        "offs2": striped(idx2),
    }


def reference(ment, ents_words, ents_scales, comp, trust, offs, offs2):
    idx = unstriped(offs)
    idx2 = unstriped(offs2)
    entsu = unpack_weight(ents_words, ents_scales, "e4m3")
    entsidxg = entsu[:, idx]
    mentq = mxq(f64(ment), 0, "e4m3")
    a = entsidxg.T @ mentq
    compidx2q = mxq(f64(comp)[:, idx2], 0, "e4m3")
    b = entsidxg.T @ compidx2q
    y = a + np.tanh(b.reshape(I, G, J // G).mean(axis=2)) * f64(trust)
    return y

@@ -1,0 +1,174 @@
+from contextlib import ExitStack
+
+import concourse.mybir as mybir
+from concourse.masks import make_identity
+
+D, T, I, J, G = 512, 2048, 512, 1024, 128
+FLOPS = 2 * D * I * (G + J)
+
+F32 = mybir.dt.float32
+BF16 = mybir.dt.bfloat16
+I32 = mybir.dt.int32
+U32 = mybir.dt.uint32
+U16 = mybir.dt.uint16
+U8 = mybir.dt.uint8
+FP8X4 = mybir.dt.float8_e4m3fn_x4
+ACT = mybir.ActivationFunctionType
+ALU = mybir.AluOpType
+
+P = 128
+COMPANIONS = J // G
+I_TILES = I // P
+CHUNKS = (((0, 1024), (1024, 2048)), ((0, 1024), (1024, 1536), (1536, 2048)))
+GATHER_SLICES = 4
+
+
+def tile_attend_coherence_kernel(tc, ment, ents_words, ents_scales, comp, trust, offs, offs2, out):
+    nc = tc.nc
+    with ExitStack() as ctx:
+        lists = ctx.enter_context(tc.tile_pool(name="lists", bufs=1))
+        sb = ctx.enter_context(tc.tile_pool(name="sb", bufs=1))
+        stage = ctx.enter_context(tc.tile_pool(name="stage", bufs=1))
+        psum = ctx.enter_context(tc.psum_pool(name="psum", bufs=1))
+
+        cand_list = lists.tile([P, I // 16], U16, name="cand_list")
+        comp_list = lists.tile([P, J // 16], U16, name="comp_list")
+
+        comp_rows = comp.rearrange("(p u e) t -> p u e t", u=2, e=2)
+        raw = {}
+
+        def load_chunk(u, n, dst):
+            c0, c1 = CHUNKS[u][n]
+            raw[u, n] = dst
+            nc.sync.dma_start(out=dst, in_=comp_rows[:, u, :, c0:c1])
+
+        pairs = [sb.tile([P, T], F32, name="pairs%d" % u) for u in range(2)]
+
+        def cast(engine, u, n, lo, hi):
+            c0 = CHUNKS[u][n][0]
+            dst = pairs[u][:, c0 + lo : c0 + hi].bitcast(BF16).rearrange("p (c e) -> p c e", e=2)
+            src = raw[u, n][:, :, lo:hi].rearrange("p e c -> p c e")
+            if engine == "scalar":
+                nc.scalar.activation(dst, src, ACT.Copy)
+            else:
+                nc.vector.tensor_copy(dst, src)
+
+        scale_pool = sb.tile([P, T], U8, name="scale_pool")
+        nc.vector.memset(scale_pool[:].bitcast(I32), 0)
+        ident = sb.tile([P, P], F32, name="ident")
+        make_identity(nc, ident[:])
+        trust_col = sb.tile([P, 1], F32, name="trust_col")
+
+        load_chunk(0, 0, stage.tile([P, 2, 1024], F32, name="raw00", offset=0)[:])
+        nc.sync.dma_start(comp_list[:], offs2)
+        nc.sync.dma_start(cand_list[:], offs)
+        nc.sync.dma_start(out=trust_col[:], in_=trust.rearrange("o g -> g o"))
+        load_chunk(0, 1, stage.tile([P, 2, 1024], F32, name="raw01", offset=8192)[:])
+        load_chunk(1, 0, stage.tile([P, 2, 1024], F32, name="raw10", offset=16384)[:])
+        for q in range(4):
+            nc.sync.dma_start(
+                out=scale_pool[32 * q : 32 * q + 4, :].bitcast(I32),
+                in_=ents_scales[0][4 * q : 4 * q + 4, :].bitcast(I32),
+            )
+
+        step = J // GATHER_SLICES
+        gs = G // GATHER_SLICES
+        picked = [sb.tile([P, 2, step], F32, name="picked%d" % s, align_bytes=64) for s in range(GATHER_SLICES)]
+
+        def pick(u, s):
+            nc.vector.tensor_copy(
+                picked[s][:, u, :],
+                pairs[u][:].indirect(comp_list[:, s * step // 16 : (s + 1) * step // 16]),
+            )
+
+        cast("scalar", 0, 0, 0, 384)
+        cast("vector", 0, 0, 384, 1024)
+        load_chunk(1, 1, stage.tile([P, 2, 512], F32, name="raw11", offset=0)[:])
+        load_chunk(1, 2, stage.tile([P, 2, 512], F32, name="raw12", offset=4096)[:])
+        cast("scalar", 0, 1, 0, 384)
+        cast("vector", 0, 1, 384, 1024)
+        word_pool = stage.tile([P, T], U32, name="word_pool", offset=8192)
+        nc.sync.dma_start(
+            out=word_pool[:].bitcast(I32),
+            in_=ents_words[0].rearrange("p n t -> p (n t)").bitcast(I32),
+        )
+
+        ment_codes = sb.tile([P, G], U32, name="ment_codes", align_bytes=64)
+        ment_scales = sb.tile([P, G], U8, name="ment_scales", align_bytes=64)
+        cand_scales = sb.tile([P, I], U8, name="cand_scales", align_bytes=64)
+        cand_words = sb.tile([P, I], U32, name="cand_words", align_bytes=64)
+
+        for s in range(GATHER_SLICES):
+            pick(0, s)
+        nc.vector.tensor_copy(cand_scales[:], scale_pool[:].indirect(cand_list[:]))
+        trust_rows = psum.tile([P, G], F32, name="trust_rows")
+        nc.tensor.transpose(trust_rows[:], trust_col[:].to_broadcast([P, P]), ident[:])
+
+        cast("scalar", 1, 0, 0, 1024)
+        ment_raw = stage.tile([P, 4, G], F32, name="ment_raw", offset=16384)
+        nc.sync.dma_start(out=ment_raw[:], in_=ment.rearrange("(p t) g -> p t g", t=4))
+        cast("vector", 1, 1, 0, 512)
+        cast("scalar", 1, 2, 0, 192)
+        cast("vector", 1, 2, 192, 512)
+
+        woven = sb.tile([P, COMPANIONS, G, 2], F32, name="woven", align_bytes=64)
+        for s in range(GATHER_SLICES):
+            pick(1, s)
+            nc.scalar.copy(
+                woven[:, :, s * gs : (s + 1) * gs, :].rearrange("p r (h e) u -> p h r e u", e=2),
+                picked[s][:].rearrange("p u (h e r) -> p h r e u", e=2, r=COMPANIONS),
+            )
+        ment_bf = sb.tile([P, G, 4], BF16, name="ment_bf", tag="picked%d" % (GATHER_SLICES - 1), align_bytes=64)
+        nc.scalar.copy(ment_bf[:], ment_raw[:].rearrange("p t g -> p g t"))
+
+        comp_codes = sb.tile([P, COMPANIONS, G], U32, name="comp_codes", align_bytes=64)
+        comp_scales = sb.tile([P, COMPANIONS, G], U8, name="comp_scales", align_bytes=64)
+        half = COMPANIONS // 2
+        for h in range(2):
+            nc.vector.tensor_copy(
+                cand_words[:, h * I // 2 : (h + 1) * I // 2],
+                word_pool[:].indirect(cand_list[:, h * I // 32 : (h + 1) * I // 32]),
+            )
+            for r in range(h * half, (h + 1) * half):
+                nc.vector.quantize_mx(
+                    out=comp_codes[:, r, :].bitcast(FP8X4),
+                    scales=comp_scales[:, r, :],
+                    in_=woven[:, r, :, :].rearrange("p g u -> p (g u)").bitcast(BF16),
+                )
+
+        nc.vector.quantize_mx(
+            out=ment_codes[:].bitcast(FP8X4),
+            scales=ment_scales[:],
+            in_=ment_bf[:].rearrange("p g t -> p (g t)"),
+        )
+        direct = psum.tile([P, I_TILES, G], F32, name="direct")
+        company = [psum.tile([P, G], F32, name="company%d" % m) for m in range(I_TILES)]
+
+        def product(dst, m, codes, scales, start, stop):
+            cols = slice(m * P, (m + 1) * P)
+            nc.tensor.matmul_mx(
+                out=dst,
+                lhsT=cand_words[:, cols].bitcast(FP8X4),
+                lhsT_scale=cand_scales[:, cols],
+                rhs=codes.bitcast(FP8X4),
+                rhs_scale=scales,
+                start=start,
+                stop=stop,
+            )
+
+        for h in range(2):
+            for r in range(half):
+                for m in (2 * h, 2 * h + 1):
+                    product(company[m][:], m, comp_codes[:, r, :], comp_scales[:, r, :], r == 0, False)
+        for m in range(I_TILES):
+            product(direct[:, m, :], m, ment_codes[:], ment_scales[:], True, True)
+        for m in range(I_TILES):
+            for r in range(half, COMPANIONS):
+                product(company[m][:], m, comp_codes[:, r, :], comp_scales[:, r, :], False, r == COMPANIONS - 1)
+            bent = sb.tile([P, G], F32, name="bent%d" % m)
+            nc.scalar.activation(bent[:], company[m][:], ACT.Tanh, scale=1.0 / COMPANIONS)
+            weighted = sb.tile([P, G], F32, name="weighted%d" % m)
+            nc.vector.tensor_tensor(weighted[:], bent[:], trust_rows[:], ALU.mult)
+            result = sb.tile([P, G], F32, name="result%d" % m)
+            nc.vector.tensor_tensor(result[:], weighted[:], direct[:, m, :], ALU.add)
+            nc.sync.dma_start(out=out[m * P : (m + 1) * P, :], in_=result[:])

@@ -17,10 +17,14 @@ ACT = mybir.ActivationFunctionType
 ALU = mybir.AluOpType
 
 P = 128
+KIB = 1024
+LIST_ROWS = 16
 COMPANIONS = J // G
+HALF = COMPANIONS // 2
 I_TILES = I // P
-CHUNKS = (((0, 1024), (1024, 2048)), ((0, 1024), (1024, 1536), (1536, 2048)))
-GATHER_SLICES = 4
+SLICES = 4
+SLICE_SLOTS = J // SLICES
+SLICE_MENTIONS = G // SLICES
 
 
 def tile_attend_coherence_kernel(tc, ment, ents_words, ents_scales, comp, trust, offs, offs2, out):
@@ -31,144 +35,165 @@ def tile_attend_coherence_kernel(tc, ment, ents_words, ents_scales, comp, trust,
         stage = ctx.enter_context(tc.tile_pool(name="stage", bufs=1))
         psum = ctx.enter_context(tc.psum_pool(name="psum", bufs=1))
 
-        cand_list = lists.tile([P, I // 16], U16, name="cand_list")
-        comp_list = lists.tile([P, J // 16], U16, name="comp_list")
+        cand_list = lists.tile([P, I // LIST_ROWS], U16, name="cand_list")
+        comp_list = lists.tile([P, J // LIST_ROWS], U16, name="comp_list")
 
         comp_rows = comp.rearrange("(p u e) t -> p u e t", u=2, e=2)
-        raw = {}
+        pairs = [sb.tile([P, 2 * T], BF16, name="pairs%d" % u, align_bytes=64) for u in range(2)]
 
-        def load_chunk(u, n, dst):
-            c0, c1 = CHUNKS[u][n]
-            raw[u, n] = dst
-            nc.sync.dma_start(out=dst, in_=comp_rows[:, u, :, c0:c1])
+        def load_chunk(u, c0, c1, offset):
+            raw = stage.tile([P, 2, c1 - c0], F32, name="raw%d_%d" % (u, c0), offset=offset)
+            nc.sync.dma_start(out=raw[:], in_=comp_rows[:, u, :, c0:c1])
+            return u, c0, c1, raw
 
-        pairs = [sb.tile([P, T], F32, name="pairs%d" % u) for u in range(2)]
-
-        def cast(engine, u, n, lo, hi):
-            c0 = CHUNKS[u][n][0]
-            dst = pairs[u][:, c0 + lo : c0 + hi].bitcast(BF16).rearrange("p (c e) -> p c e", e=2)
-            src = raw[u, n][:, :, lo:hi].rearrange("p e c -> p c e")
-            if engine == "scalar":
-                nc.scalar.activation(dst, src, ACT.Copy)
-            else:
-                nc.vector.tensor_copy(dst, src)
+        def cast(chunk, scalar_columns):
+            u, c0, c1, raw = chunk
+            cut = c0 + scalar_columns
+            src = raw[:].rearrange("p e c -> p c e")
+            if cut < c1:
+                dst = pairs[u][:, 2 * cut : 2 * c1].rearrange("p (c e) -> p c e", e=2)
+                nc.vector.tensor_copy(dst, src[:, scalar_columns:])
+            if cut > c0:
+                dst = pairs[u][:, 2 * c0 : 2 * cut].rearrange("p (c e) -> p c e", e=2)
+                nc.scalar.activation(dst, src[:, :scalar_columns], ACT.Copy)
 
         scale_pool = sb.tile([P, T], U8, name="scale_pool")
         nc.vector.memset(scale_pool[:].bitcast(I32), 0)
+        trust_row = sb.tile([P, G], F32, name="trust_row")
+        nc.gpsimd.memset(trust_row[:], 0.0)
         ident = sb.tile([P, P], F32, name="ident")
         make_identity(nc, ident[:])
-        trust_col = sb.tile([P, 1], F32, name="trust_col")
 
-        load_chunk(0, 0, stage.tile([P, 2, 1024], F32, name="raw00", offset=0)[:])
-        nc.sync.dma_start(comp_list[:], offs2)
+        first0 = load_chunk(0, 0, 512, 0)
         nc.sync.dma_start(cand_list[:], offs)
-        nc.sync.dma_start(out=trust_col[:], in_=trust.rearrange("o g -> g o"))
-        load_chunk(0, 1, stage.tile([P, 2, 1024], F32, name="raw01", offset=8192)[:])
-        load_chunk(1, 0, stage.tile([P, 2, 1024], F32, name="raw10", offset=16384)[:])
+        nc.sync.dma_start(comp_list[:], offs2)
+        middle0 = load_chunk(0, 512, 1536, 8 * KIB)
+        last0 = load_chunk(0, 1536, 2048, 16 * KIB)
+        nc.sync.dma_start(out=trust_row[0:1, :], in_=trust)
         for q in range(4):
             nc.sync.dma_start(
                 out=scale_pool[32 * q : 32 * q + 4, :].bitcast(I32),
                 in_=ents_scales[0][4 * q : 4 * q + 4, :].bitcast(I32),
             )
 
-        step = J // GATHER_SLICES
-        gs = G // GATHER_SLICES
-        picked = [sb.tile([P, 2, step], F32, name="picked%d" % s, align_bytes=64) for s in range(GATHER_SLICES)]
-
-        def pick(u, s):
-            nc.vector.tensor_copy(
-                picked[s][:, u, :],
-                pairs[u][:].indirect(comp_list[:, s * step // 16 : (s + 1) * step // 16]),
-            )
-
-        cast("scalar", 0, 0, 0, 384)
-        cast("vector", 0, 0, 384, 1024)
-        load_chunk(1, 1, stage.tile([P, 2, 512], F32, name="raw11", offset=0)[:])
-        load_chunk(1, 2, stage.tile([P, 2, 512], F32, name="raw12", offset=4096)[:])
-        cast("scalar", 0, 1, 0, 384)
-        cast("vector", 0, 1, 384, 1024)
-        word_pool = stage.tile([P, T], U32, name="word_pool", offset=8192)
+        cast(first0, 160)
+        first1 = load_chunk(1, 0, 1024, 0)
+        cast(middle0, 352)
+        middle1 = load_chunk(1, 1024, 1664, 8 * KIB)
+        last1 = load_chunk(1, 1664, 2048, 13 * KIB)
+        cast(last0, 160)
+        word_pool = stage.tile([P, T], U32, name="word_pool", offset=16 * KIB + 64)
         nc.sync.dma_start(
             out=word_pool[:].bitcast(I32),
             in_=ents_words[0].rearrange("p n t -> p (n t)").bitcast(I32),
         )
 
-        ment_codes = sb.tile([P, G], U32, name="ment_codes", align_bytes=64)
-        ment_scales = sb.tile([P, G], U8, name="ment_scales", align_bytes=64)
+        picked = sb.tile([P, 2, J], F32, name="picked", align_bytes=64)
+        nc.vector.tensor_copy(picked[:, 0, :], pairs[0][:].bitcast(F32).indirect(comp_list[:]))
         cand_scales = sb.tile([P, I], U8, name="cand_scales", align_bytes=64)
-        cand_words = sb.tile([P, I], U32, name="cand_words", align_bytes=64)
-
-        for s in range(GATHER_SLICES):
-            pick(0, s)
         nc.vector.tensor_copy(cand_scales[:], scale_pool[:].indirect(cand_list[:]))
+
+        cast(first1, 1024)
+        ment_raw = stage.tile([P, 4, G], F32, name="ment_raw", offset=0)
+        nc.sync.dma_start(out=ment_raw[:], in_=ment.rearrange("(p t) g -> p t g", t=4))
+
+        trust_turned = psum.tile([P, P], F32, name="trust_turned")
+        nc.tensor.transpose(trust_turned[:], trust_row[:], ident[:])
+        trust_col = stage.tile([P, 1], F32, name="trust_col", offset=16 * KIB)
+        nc.scalar.copy(trust_col[:], trust_turned[:, 0:1])
         trust_rows = psum.tile([P, G], F32, name="trust_rows")
         nc.tensor.transpose(trust_rows[:], trust_col[:].to_broadcast([P, P]), ident[:])
 
-        cast("scalar", 1, 0, 0, 1024)
-        ment_raw = stage.tile([P, 4, G], F32, name="ment_raw", offset=16384)
-        nc.sync.dma_start(out=ment_raw[:], in_=ment.rearrange("(p t) g -> p t g", t=4))
-        cast("vector", 1, 1, 0, 512)
-        cast("scalar", 1, 2, 0, 192)
-        cast("vector", 1, 2, 192, 512)
+        cast(middle1, 0)
+        cast(last1, 128)
 
-        woven = sb.tile([P, COMPANIONS, G, 2], F32, name="woven", align_bytes=64)
-        for s in range(GATHER_SLICES):
-            pick(1, s)
+        dealt = [sb.tile([P, HALF, G, 2], F32, name="dealt%d" % h, align_bytes=64) for h in range(2)]
+
+        def deal(s, h):
+            slots = slice(s * SLICE_SLOTS, (s + 1) * SLICE_SLOTS)
+            mentions = slice(s * SLICE_MENTIONS, (s + 1) * SLICE_MENTIONS)
+            by_companion = picked[:, :, slots].rearrange("p u (c e r) -> p c r e u", e=2, r=COMPANIONS)
             nc.scalar.copy(
-                woven[:, :, s * gs : (s + 1) * gs, :].rearrange("p r (h e) u -> p h r e u", e=2),
-                picked[s][:].rearrange("p u (h e r) -> p h r e u", e=2, r=COMPANIONS),
+                dealt[h][:, :, mentions, :].rearrange("p r (c e) u -> p c r e u", e=2),
+                by_companion[:, :, h * HALF : (h + 1) * HALF],
             )
-        ment_bf = sb.tile([P, G, 4], BF16, name="ment_bf", tag="picked%d" % (GATHER_SLICES - 1), align_bytes=64)
+
+        for s in range(SLICES):
+            nc.vector.tensor_copy(
+                picked[:, 1, s * SLICE_SLOTS : (s + 1) * SLICE_SLOTS],
+                pairs[1][:]
+                .bitcast(F32)
+                .indirect(comp_list[:, s * SLICE_SLOTS // LIST_ROWS : (s + 1) * SLICE_SLOTS // LIST_ROWS]),
+            )
+            deal(s, 0)
+            if s < SLICES - 2:
+                deal(s, 1)
+        for s in range(SLICES - 2, SLICES):
+            deal(s, 1)
+        ment_bf = sb.tile([P, G, 4], BF16, name="ment_bf", tag="picked", align_bytes=64)
         nc.scalar.copy(ment_bf[:], ment_raw[:].rearrange("p t g -> p g t"))
 
-        comp_codes = sb.tile([P, COMPANIONS, G], U32, name="comp_codes", align_bytes=64)
-        comp_scales = sb.tile([P, COMPANIONS, G], U8, name="comp_scales", align_bytes=64)
-        half = COMPANIONS // 2
-        for h in range(2):
-            nc.vector.tensor_copy(
-                cand_words[:, h * I // 2 : (h + 1) * I // 2],
-                word_pool[:].indirect(cand_list[:, h * I // 32 : (h + 1) * I // 32]),
-            )
-            for r in range(h * half, (h + 1) * half):
-                nc.vector.quantize_mx(
-                    out=comp_codes[:, r, :].bitcast(FP8X4),
-                    scales=comp_scales[:, r, :],
-                    in_=woven[:, r, :, :].rearrange("p g u -> p (g u)").bitcast(BF16),
-                )
+        def gather_words(h, tag):
+            words = sb.tile([P, I // 2], U32, name="cand_words%d" % h, tag=tag, align_bytes=64)
+            columns = I // 2 // LIST_ROWS
+            nc.vector.tensor_copy(words[:], word_pool[:].indirect(cand_list[:, h * columns : (h + 1) * columns]))
+            return words
 
-        nc.vector.quantize_mx(
-            out=ment_codes[:].bitcast(FP8X4),
-            scales=ment_scales[:],
-            in_=ment_bf[:].rearrange("p g t -> p (g t)"),
-        )
-        direct = psum.tile([P, I_TILES, G], F32, name="direct")
+        def quantize(name, values, columns):
+            codes = sb.tile([P, columns], U32, name=name + "_codes", align_bytes=64)
+            scales = sb.tile([P, columns], U8, name=name + "_scales", align_bytes=64)
+            nc.vector.quantize_mx(out=codes[:].bitcast(FP8X4), scales=scales[:], in_=values)
+            return codes, scales
+
+        cand_words = [gather_words(0, "pairs1")]
+        comp_mx = []
+        for r, n in ((0, 1), (1, 1), (2, 2), (4, 2), (6, 2)):
+            values = dealt[r // HALF][:, r % HALF : r % HALF + n].rearrange("p r g u -> p (r g u)").bitcast(BF16)
+            codes, scales = quantize("comp%d" % r, values, n * G)
+            comp_mx.extend((codes[:, e * G : (e + 1) * G], scales[:, e * G : (e + 1) * G]) for e in range(n))
+        ment_codes, ment_scales = quantize("ment", ment_bf[:].rearrange("p g t -> p (g t)"), G)
+        cand_words.append(gather_words(1, "dealt1"))
+
+        direct = [psum.tile([P, 2, G], F32, name="direct%d" % h) for h in range(2)]
         company = [psum.tile([P, G], F32, name="company%d" % m) for m in range(I_TILES)]
 
         def product(dst, m, codes, scales, start, stop):
-            cols = slice(m * P, (m + 1) * P)
             nc.tensor.matmul_mx(
                 out=dst,
-                lhsT=cand_words[:, cols].bitcast(FP8X4),
-                lhsT_scale=cand_scales[:, cols],
+                lhsT=cand_words[m // 2][:, (m % 2) * P : (m % 2 + 1) * P].bitcast(FP8X4),
+                lhsT_scale=cand_scales[:, m * P : (m + 1) * P],
                 rhs=codes.bitcast(FP8X4),
                 rhs_scale=scales,
                 start=start,
                 stop=stop,
             )
 
-        for h in range(2):
-            for r in range(half):
-                for m in (2 * h, 2 * h + 1):
-                    product(company[m][:], m, comp_codes[:, r, :], comp_scales[:, r, :], r == 0, False)
-        for m in range(I_TILES):
-            product(direct[:, m, :], m, ment_codes[:], ment_scales[:], True, True)
-        for m in range(I_TILES):
-            for r in range(half, COMPANIONS):
-                product(company[m][:], m, comp_codes[:, r, :], comp_scales[:, r, :], False, r == COMPANIONS - 1)
+        def company_pass(m, r):
+            product(company[m][:], m, comp_mx[r][0], comp_mx[r][1], r == 0, r == COMPANIONS - 1)
+
+        def direct_pass(m):
+            product(direct[m // 2][:, m % 2, :], m, ment_codes[:], ment_scales[:], True, True)
+
+        def finish(m):
             bent = sb.tile([P, G], F32, name="bent%d" % m)
             nc.scalar.activation(bent[:], company[m][:], ACT.Tanh, scale=1.0 / COMPANIONS)
             weighted = sb.tile([P, G], F32, name="weighted%d" % m)
             nc.vector.tensor_tensor(weighted[:], bent[:], trust_rows[:], ALU.mult)
             result = sb.tile([P, G], F32, name="result%d" % m)
-            nc.vector.tensor_tensor(result[:], weighted[:], direct[:, m, :], ALU.add)
+            nc.vector.tensor_tensor(result[:], weighted[:], direct[m // 2][:, m % 2, :], ALU.add)
             nc.sync.dma_start(out=out[m * P : (m + 1) * P, :], in_=result[:])
+
+        for r in range(HALF):
+            for m in (0, 1):
+                company_pass(m, r)
+        for m in (0, 1):
+            for r in range(HALF, COMPANIONS):
+                company_pass(m, r)
+        for m in range(I_TILES):
+            direct_pass(m)
+        finish(0)
+        finish(1)
+        for m in (2, 3):
+            for r in range(COMPANIONS):
+                company_pass(m, r)
+            finish(m)

from contextlib import ExitStack

import concourse.mybir as mybir
from concourse.masks import make_identity

D, T, I, J, G = 512, 2048, 512, 1024, 128
FLOPS = 2 * D * I * (G + J)

F32 = mybir.dt.float32
BF16 = mybir.dt.bfloat16
I32 = mybir.dt.int32
U32 = mybir.dt.uint32
U16 = mybir.dt.uint16
U8 = mybir.dt.uint8
FP8X4 = mybir.dt.float8_e4m3fn_x4
ACT = mybir.ActivationFunctionType
ALU = mybir.AluOpType

P = 128
KIB = 1024
LIST_ROWS = 16
COMPANIONS = J // G
HALF = COMPANIONS // 2
I_TILES = I // P
SLICES = 4
SLICE_SLOTS = J // SLICES
SLICE_MENTIONS = G // SLICES


def tile_attend_coherence_kernel(tc, ment, ents_words, ents_scales, comp, trust, offs, offs2, out):
    nc = tc.nc
    with ExitStack() as ctx:
        lists = ctx.enter_context(tc.tile_pool(name="lists", bufs=1))
        sb = ctx.enter_context(tc.tile_pool(name="sb", bufs=1))
        stage = ctx.enter_context(tc.tile_pool(name="stage", bufs=1))
        psum = ctx.enter_context(tc.psum_pool(name="psum", bufs=1))

        cand_list = lists.tile([P, I // LIST_ROWS], U16, name="cand_list")
        comp_list = lists.tile([P, J // LIST_ROWS], U16, name="comp_list")

        comp_rows = comp.rearrange("(p u e) t -> p u e t", u=2, e=2)
        pairs = [sb.tile([P, 2 * T], BF16, name="pairs%d" % u, align_bytes=64) for u in range(2)]

        def load_chunk(u, c0, c1, offset):
            raw = stage.tile([P, 2, c1 - c0], F32, name="raw%d_%d" % (u, c0), offset=offset)
            nc.sync.dma_start(out=raw[:], in_=comp_rows[:, u, :, c0:c1])
            return u, c0, c1, raw

        def cast(chunk, scalar_columns):
            u, c0, c1, raw = chunk
            cut = c0 + scalar_columns
            src = raw[:].rearrange("p e c -> p c e")
            if cut < c1:
                dst = pairs[u][:, 2 * cut : 2 * c1].rearrange("p (c e) -> p c e", e=2)
                nc.vector.tensor_copy(dst, src[:, scalar_columns:])
            if cut > c0:
                dst = pairs[u][:, 2 * c0 : 2 * cut].rearrange("p (c e) -> p c e", e=2)
                nc.scalar.activation(dst, src[:, :scalar_columns], ACT.Copy)

        scale_pool = sb.tile([P, T], U8, name="scale_pool")
        nc.vector.memset(scale_pool[:].bitcast(I32), 0)
        trust_row = sb.tile([P, G], F32, name="trust_row")
        nc.gpsimd.memset(trust_row[:], 0.0)
        ident = sb.tile([P, P], F32, name="ident")
        make_identity(nc, ident[:])

        first0 = load_chunk(0, 0, 512, 0)
        nc.sync.dma_start(cand_list[:], offs)
        nc.sync.dma_start(comp_list[:], offs2)
        middle0 = load_chunk(0, 512, 1536, 8 * KIB)
        last0 = load_chunk(0, 1536, 2048, 16 * KIB)
        nc.sync.dma_start(out=trust_row[0:1, :], in_=trust)
        for q in range(4):
            nc.sync.dma_start(
                out=scale_pool[32 * q : 32 * q + 4, :].bitcast(I32),
                in_=ents_scales[0][4 * q : 4 * q + 4, :].bitcast(I32),
            )

        cast(first0, 160)
        first1 = load_chunk(1, 0, 1024, 0)
        cast(middle0, 352)
        middle1 = load_chunk(1, 1024, 1664, 8 * KIB)
        last1 = load_chunk(1, 1664, 2048, 13 * KIB)
        cast(last0, 160)
        word_pool = stage.tile([P, T], U32, name="word_pool", offset=16 * KIB + 64)
        nc.sync.dma_start(
            out=word_pool[:].bitcast(I32),
            in_=ents_words[0].rearrange("p n t -> p (n t)").bitcast(I32),
        )

        picked = sb.tile([P, 2, J], F32, name="picked", align_bytes=64)
        nc.vector.tensor_copy(picked[:, 0, :], pairs[0][:].bitcast(F32).indirect(comp_list[:]))
        cand_scales = sb.tile([P, I], U8, name="cand_scales", align_bytes=64)
        nc.vector.tensor_copy(cand_scales[:], scale_pool[:].indirect(cand_list[:]))

        cast(first1, 1024)
        ment_raw = stage.tile([P, 4, G], F32, name="ment_raw", offset=0)
        nc.sync.dma_start(out=ment_raw[:], in_=ment.rearrange("(p t) g -> p t g", t=4))

        trust_turned = psum.tile([P, P], F32, name="trust_turned")
        nc.tensor.transpose(trust_turned[:], trust_row[:], ident[:])
        trust_col = stage.tile([P, 1], F32, name="trust_col", offset=16 * KIB)
        nc.scalar.copy(trust_col[:], trust_turned[:, 0:1])
        trust_rows = psum.tile([P, G], F32, name="trust_rows")
        nc.tensor.transpose(trust_rows[:], trust_col[:].to_broadcast([P, P]), ident[:])

        cast(middle1, 0)
        cast(last1, 128)

        dealt = [sb.tile([P, HALF, G, 2], F32, name="dealt%d" % h, align_bytes=64) for h in range(2)]

        def deal(s, h):
            slots = slice(s * SLICE_SLOTS, (s + 1) * SLICE_SLOTS)
            mentions = slice(s * SLICE_MENTIONS, (s + 1) * SLICE_MENTIONS)
            by_companion = picked[:, :, slots].rearrange("p u (c e r) -> p c r e u", e=2, r=COMPANIONS)
            nc.scalar.copy(
                dealt[h][:, :, mentions, :].rearrange("p r (c e) u -> p c r e u", e=2),
                by_companion[:, :, h * HALF : (h + 1) * HALF],
            )

        for s in range(SLICES):
            nc.vector.tensor_copy(
                picked[:, 1, s * SLICE_SLOTS : (s + 1) * SLICE_SLOTS],
                pairs[1][:]
                .bitcast(F32)
                .indirect(comp_list[:, s * SLICE_SLOTS // LIST_ROWS : (s + 1) * SLICE_SLOTS // LIST_ROWS]),
            )
            deal(s, 0)
            if s < SLICES - 2:
                deal(s, 1)
        for s in range(SLICES - 2, SLICES):
            deal(s, 1)
        ment_bf = sb.tile([P, G, 4], BF16, name="ment_bf", tag="picked", align_bytes=64)
        nc.scalar.copy(ment_bf[:], ment_raw[:].rearrange("p t g -> p g t"))

        def gather_words(h, tag):
            words = sb.tile([P, I // 2], U32, name="cand_words%d" % h, tag=tag, align_bytes=64)
            columns = I // 2 // LIST_ROWS
            nc.vector.tensor_copy(words[:], word_pool[:].indirect(cand_list[:, h * columns : (h + 1) * columns]))
            return words

        def quantize(name, values, columns):
            codes = sb.tile([P, columns], U32, name=name + "_codes", align_bytes=64)
            scales = sb.tile([P, columns], U8, name=name + "_scales", align_bytes=64)
            nc.vector.quantize_mx(out=codes[:].bitcast(FP8X4), scales=scales[:], in_=values)
            return codes, scales

        cand_words = [gather_words(0, "pairs1")]
        comp_mx = []
        for r, n in ((0, 1), (1, 1), (2, 2), (4, 2), (6, 2)):
            values = dealt[r // HALF][:, r % HALF : r % HALF + n].rearrange("p r g u -> p (r g u)").bitcast(BF16)
            codes, scales = quantize("comp%d" % r, values, n * G)
            comp_mx.extend((codes[:, e * G : (e + 1) * G], scales[:, e * G : (e + 1) * G]) for e in range(n))
        ment_codes, ment_scales = quantize("ment", ment_bf[:].rearrange("p g t -> p (g t)"), G)
        cand_words.append(gather_words(1, "dealt1"))

        direct = [psum.tile([P, 2, G], F32, name="direct%d" % h) for h in range(2)]
        company = [psum.tile([P, G], F32, name="company%d" % m) for m in range(I_TILES)]

        def product(dst, m, codes, scales, start, stop):
            nc.tensor.matmul_mx(
                out=dst,
                lhsT=cand_words[m // 2][:, (m % 2) * P : (m % 2 + 1) * P].bitcast(FP8X4),
                lhsT_scale=cand_scales[:, m * P : (m + 1) * P],
                rhs=codes.bitcast(FP8X4),
                rhs_scale=scales,
                start=start,
                stop=stop,
            )

        def company_pass(m, r):
            product(company[m][:], m, comp_mx[r][0], comp_mx[r][1], r == 0, r == COMPANIONS - 1)

        def direct_pass(m):
            product(direct[m // 2][:, m % 2, :], m, ment_codes[:], ment_scales[:], True, True)

        def finish(m):
            bent = sb.tile([P, G], F32, name="bent%d" % m)
            nc.scalar.activation(bent[:], company[m][:], ACT.Tanh, scale=1.0 / COMPANIONS)
            weighted = sb.tile([P, G], F32, name="weighted%d" % m)
            nc.vector.tensor_tensor(weighted[:], bent[:], trust_rows[:], ALU.mult)
            result = sb.tile([P, G], F32, name="result%d" % m)
            nc.vector.tensor_tensor(result[:], weighted[:], direct[m // 2][:, m % 2, :], ALU.add)
            nc.sync.dma_start(out=out[m * P : (m + 1) * P, :], in_=result[:])

        for r in range(HALF):
            for m in (0, 1):
                company_pass(m, r)
        for m in (0, 1):
            for r in range(HALF, COMPANIONS):
                company_pass(m, r)
        for m in range(I_TILES):
            direct_pass(m)
        finish(0)
        finish(1)
        for m in (2, 3):
            for r in range(COMPANIONS):
                company_pass(m, r)
            finish(m)
